import numpy as np
import ml_dtypes


def mxq(x, axis, fmt="e4m3"):
    dtype, down = {"e4m3": (ml_dtypes.float8_e4m3fn, 7), "e5m2": (ml_dtypes.float8_e5m2, 14)}[fmt]
    v = np.moveaxis(np.asarray(x, np.float32).astype(ml_dtypes.bfloat16).astype(np.float64), axis, -1)
    blocks = v.reshape(v.shape[:-1] + (-1, 32))
    amax = np.abs(blocks).max(-1, keepdims=True)
    byte = np.maximum(np.where(amax > 0, np.frexp(amax)[1] - 1 + 127, 0) - down, 1)
    scale = np.exp2(byte - 127.0)
    codes = (blocks / scale).astype(np.float32).astype(dtype).astype(np.float64)
    return np.moveaxis((codes * scale).reshape(v.shape), -1, axis)


WIDE = False


def mx_kscale(k):
    if not WIDE:
        return np.ones(k)
    levels = np.array([10, -10, 5, -5, 0])
    if k % 512:
        return np.exp2(np.random.permutation(np.resize(levels, k // 32))).repeat(32)
    a = np.empty((k // 512, 16))
    for p in range(k // 512):
        a[p, :8] = np.random.permutation(np.resize(levels, 8))
        for g in range(8):
            far = levels[np.abs(levels - a[p, g]) >= 10]
            a[p, g + 8] = far[np.random.randint(len(far))]
    return np.exp2(a.ravel()).repeat(32)


def f64(x):
    return np.asarray(x).astype(np.float64)


def striped(idx):
    return np.tile(idx.reshape(-1, 16).T, (8, 1)).astype(np.uint16)


def unstriped(offs):
    return offs[:16].T.reshape(-1).astype(np.int64)


def striped8(idx):
    return np.concatenate([x.reshape(-1, 16).T for x in idx]).astype(np.uint16)


def runs(offs, k):
    lists = np.stack([offs[16 * r : 16 * r + 16].T.reshape(-1) for r in range(8)]).astype(np.int64)
    return lists[np.arange(k) % 512 // 64]


def pack_weight(w):
    k, n = w.shape
    w = f64(np.asarray(w, np.float32).astype(ml_dtypes.bfloat16)).reshape(k // 32, 32, n)
    amax = np.abs(w).max(1)
    byte = np.clip(np.where(amax > 0, np.frexp(amax)[1] - 1 + 127 - 7, 1), 1, 254)
    scaled = (w * np.exp2(127.0 - byte)[:, None, :]).reshape(k, n).astype(np.float32)
    words = np.ascontiguousarray(scaled.reshape(k // 512, 128, 4, n).transpose(0, 1, 3, 2)).astype(ml_dtypes.float8_e4m3fn).view(np.uint8)
    return words, np.ascontiguousarray(byte.astype(np.uint8).reshape(k // 512, 16, n))


def unpack_weight(words, scales):
    g, p, n, _ = words.shape
    vals = np.ascontiguousarray(words).view(ml_dtypes.float8_e4m3fn).astype(np.float64) * np.repeat(np.exp2(scales.astype(np.float64) - 127.0), 8, axis=1)[..., None]
    return vals.transpose(0, 1, 3, 2).reshape(g * 512, n)


def sigmoid(v):
    return 1.0 / (1.0 + np.exp(-np.maximum(v, -700.0)))

def planes(y):
    n, m = y.shape
    v = y.astype(np.float32).astype(ml_dtypes.bfloat16).astype(np.float64).reshape(n // 32, 32, m)
    top = np.abs(v).max(1)
    byte = np.clip(np.where(top > 0, np.frexp(top)[1] - 1 + 127 - 7, 1), 1, 254)
    codes = (v * np.exp2(127.0 - byte)[:, None, :]).reshape(n, m).astype(np.float32).astype(ml_dtypes.float8_e4m3fn).view(np.uint8)
    words = codes.reshape(n // 512, 128, 4, m).transpose(0, 1, 3, 2)
    return np.ascontiguousarray(words), np.ascontiguousarray(byte.astype(np.uint8).reshape(n // 512, 16, m))


K, T, S, V, H, C = 512, 2048, 1024, 512, 512, 512


def setup_inputs():
    n = np.random.standard_normal
    s = mx_kscale(K)[:, None]
    packed_xT = pack_weight(n((K, T)) * s)
    packed_w1 = pack_weight(n((K, H)) / np.sqrt(K) / s)
    return {
        "x_words": packed_xT[0],
        "x_scales": packed_xT[1],
        "w1_words": packed_w1[0],
        "w1_scales": packed_w1[1],
        "gs": (np.random.uniform(0.5, 1.5, (K, 1)) / s).astype(np.float32),
        "offs": striped(np.random.permutation(T)[:S]),
        "n1": striped8(np.stack([np.random.permutation(S) for _ in range(8)])),
        "cand": striped(np.random.permutation(T)[:C]),
        "n2": striped8(np.stack([np.random.permutation(V) for _ in range(8)])),
    }


def reference(x_words, x_scales, w1_words, w1_scales, gs, offs, n1, cand, n2):
    x_cand = unpack_weight(x_words, x_scales)[:, unstriped(cand)]
    xq = unpack_weight(x_words, x_scales)[:, unstriped(offs)]
    y = unpack_weight(w1_words, w1_scales).T @ xq
    ln = y[np.arange(H)[:, None], runs(n1, H)]
    sq = (ln) ** 2
    ms = sq.reshape(H, V, 2).sum(axis=2)
    z = f64(gs) * np.sqrt(ms + 0.1)
    s = 0.0625 * ((x_cand.T @ mxq(z, 0, "e4m3")))
    st = s * (sigmoid(s[np.arange(C)[:, None], runs(n2, C)]))
    out_0 = np.maximum(st, st[np.arange(C)[:, None], runs(n2, C)])
    return (out_0,) + planes(out_0)

@@ -1,0 +1,260 @@
+from contextlib import ExitStack
+
+import concourse.mybir as mybir
+
+K, T, S, V, H, C = 512, 2048, 1024, 512, 512, 512
+FLOPS = 2 * K * H * S + 2 * K * C * V
+
+F32 = mybir.dt.float32
+BF16 = mybir.dt.bfloat16
+I32 = mybir.dt.int32
+U32 = mybir.dt.uint32
+U16 = mybir.dt.uint16
+U8 = mybir.dt.uint8
+FP8X4 = mybir.dt.float8_e4m3fn_x4
+ACT = mybir.ActivationFunctionType
+ALU = mybir.AluOpType
+
+P = 128
+PACK = 4
+LIST_ROWS = 16
+HALVES = 2
+SH = S // HALVES
+VH = V // HALVES
+
+
+def entries(lst, first, count):
+    return lst[:, first // LIST_ROWS : (first + count) // LIST_ROWS]
+
+
+def tile_picked_candprmstwicp_none_po_kernel(
+    tc, x_words, x_scales, w1_words, w1_scales, gs, offs, n1, cand, n2, out_0, out_1, out_2
+):
+    nc = tc.nc
+    with ExitStack() as ctx:
+        held = ctx.enter_context(tc.tile_pool(name="held", bufs=1))
+        ring = ctx.enter_context(tc.tile_pool(name="ring", bufs=3))
+        psum = ctx.enter_context(tc.psum_pool(name="psum", bufs=8))
+
+        def keep(name, shape, dtype, tag=None):
+            return held.tile(shape, dtype, name=name, tag=tag or name, align_bytes=64)
+
+        offs_sb = held.tile([P, S // LIST_ROWS], U16, name="offs_sb")
+        n1_sb = held.tile([P, S // LIST_ROWS], U16, name="n1_sb")
+        cand_sb = held.tile([P, C // LIST_ROWS], U16, name="cand_sb")
+        n2_sb = held.tile([P, V // LIST_ROWS], U16, name="n2_sb")
+        xw = keep("xw", [P, T], U32)
+        xs = keep("xs", [P, T], U8)
+        ww = keep("ww", [P, H], U32)
+        ws = keep("ws", [P, H], U8, "slot_a")
+        gs_sb = keep("gs_sb", [P, PACK], F32)
+
+        def load_scale_rows(queues, tile, scales):
+            for q in range(4):
+                queues[q].dma_start(
+                    out=tile[32 * q : 32 * q + 4, :].bitcast(I32),
+                    in_=scales[0, 4 * q : 4 * q + 4, :].bitcast(I32),
+                )
+
+        def words_of(dram):
+            return dram[0].rearrange("p n t -> p (n t)").bitcast(I32)
+
+        nc.vector.memset(xs[:].bitcast(I32), 0)
+        nc.vector.memset(ws[:].bitcast(I32), 0)
+        nc.sync.dma_start(offs_sb[:], offs)
+        nc.sync.dma_start(cand_sb[:], cand)
+        nc.sync.dma_start(n1_sb[:], n1)
+        nc.sync.dma_start(n2_sb[:], n2)
+        nc.sync.dma_start(out=xw[:].bitcast(I32), in_=words_of(x_words))
+        nc.sync.dma_start(out=ww[:].bitcast(I32), in_=words_of(w1_words))
+        load_scale_rows([nc.scalar] * 4, xs, x_scales)
+        load_scale_rows([nc.scalar, nc.scalar, nc.gpsimd, nc.gpsimd], ws, w1_scales)
+        nc.gpsimd.dma_start(out=gs_sb[:], in_=gs.rearrange("(p t) o -> p (t o)", t=PACK))
+
+        pick_s = keep("pick_s", [P, S], U8)
+        nc.vector.tensor_copy(pick_s[:], xs[:].indirect(offs_sb[:]))
+        w_words = keep("w_words", [P, H], U32)
+        w_scales = keep("w_scales", [P, H], U8)
+        nc.vector.tensor_copy(
+            w_words[:].bitcast(I32).rearrange("p (t m) -> p t m", t=PACK),
+            ww[:].bitcast(I32).rearrange("p (m t) -> p t m", t=PACK),
+        )
+        nc.vector.tensor_copy(
+            w_scales[:].rearrange("p (t m) -> p t m", t=PACK),
+            ws[:].rearrange("p (m t) -> p t m", t=PACK),
+        )
+        pick_w = [keep("pick_w0", [P, SH], U32), keep("pick_w1", [P, SH], U32)]
+        for h in range(HALVES):
+            nc.vector.tensor_copy(pick_w[h][:], xw[:].indirect(entries(offs_sb, h * SH, SH)))
+
+        ysq = [keep("ysq%d" % t, [P, S], F32) for t in range(PACK)]
+        for t in range(PACK):
+            rows = slice(t * P, (t + 1) * P)
+            for h in range(HALVES):
+                cols = slice(h * SH, (h + 1) * SH)
+                bank = psum.tile([P, SH], F32, name="bank")
+                nc.tensor.matmul_mx(
+                    out=bank[:],
+                    lhsT=w_words[:, rows].bitcast(FP8X4),
+                    lhsT_scale=w_scales[:, rows],
+                    rhs=pick_w[h][:].bitcast(FP8X4),
+                    rhs_scale=pick_s[:, cols],
+                    start=True,
+                    stop=True,
+                )
+                nc.scalar.activation(out=ysq[t][:, cols], in_=bank[:], func=ACT.Square)
+
+        cand_s_raw = keep("cand_s_raw", [P, C], U8, "slot_a")
+        cand_s = keep("cand_s", [P, C], U8)
+        nc.vector.tensor_copy(cand_s_raw[:], xs[:].indirect(cand_sb[:]))
+
+        z_words = [keep("z_words%d" % h, [P, VH], U32) for h in range(HALVES)]
+        z_scales = [keep("z_scales%d" % h, [P, VH], U8) for h in range(HALVES)]
+        ms = [keep("ms%d" % h, [P, PACK, VH], F32) for h in range(HALVES)]
+        root = [keep("root%d" % h, [P, VH, PACK], F32) for h in range(HALVES)]
+        z_bf = [keep("z_bf%d" % h, [P, VH, PACK], BF16) for h in range(HALVES)]
+
+        def line_up(h, t):
+            if (h, t) == (HALVES - 1, PACK - 1):
+                lined = keep("last_lined", [P, SH], F32, "slot_c")
+            else:
+                lined = ring.tile([P, SH], F32, name="lined")
+            nc.vector.tensor_copy(lined[:], ysq[t][:].indirect(entries(n1_sb, h * SH, SH)))
+            return lined
+
+        def pair_sum(h, t, lined):
+            pairs = lined[:].rearrange("p (v two) -> p v two", two=2)
+            nc.vector.scalar_tensor_tensor(
+                out=ms[h][:, t, :], in0=pairs[:, :, 0], scalar=0.1, in1=pairs[:, :, 1], op0=ALU.add, op1=ALU.add
+            )
+
+        def take_root(h):
+            nc.scalar.activation(out=root[h][:], in_=ms[h][:].rearrange("p t v -> p v t"), func=ACT.Sqrt)
+
+        def weigh(h):
+            nc.vector.tensor_tensor(
+                out=z_bf[h][:], in0=root[h][:], in1=gs_sb[:].unsqueeze(1).to_broadcast([P, VH, PACK]), op=ALU.mult
+            )
+
+        def quantize_z(h):
+            nc.vector.quantize_mx(
+                out=z_words[h][:].bitcast(FP8X4), scales=z_scales[h][:], in_=z_bf[h][:].rearrange("p v t -> p (v t)")
+            )
+
+        steps = [(h, t) for h in range(HALVES) for t in range(PACK)]
+        before = None
+        for h, t in steps:
+            lined = line_up(h, t)
+            if (h, t) == (0, 0):
+                nc.vector.tensor_copy(
+                    cand_s[:].rearrange("p (t m) -> p t m", t=PACK),
+                    cand_s_raw[:].rearrange("p (m t) -> p t m", t=PACK),
+                )
+            if before is not None:
+                pair_sum(*before)
+                if before[1] == PACK - 1:
+                    take_root(before[0])
+            if (h, t) == (1, 2):
+                weigh(0)
+            if (h, t) == (1, 3):
+                quantize_z(0)
+            before = (h, t, lined)
+        pair_sum(*before)
+        take_root(1)
+        cand_w = keep("cand_w", [P, C], U32, "slot_c")
+        nc.vector.tensor_copy(cand_w[:].rearrange("p (t m) -> p m t", t=PACK), xw[:].indirect(cand_sb[:]))
+        weigh(1)
+        quantize_z(1)
+
+        score = [keep("score%d" % t, [P, V], F32) for t in range(PACK)]
+        gate = [keep("gate%d" % t, [P, V], F32) for t in range(PACK)]
+        st = [keep("st%d" % t, [P, V], F32) for t in range(PACK)]
+        res = [keep("res%d" % h, [P, PACK, VH], F32) for h in range(HALVES)]
+        res_bf = [keep("res_bf%d" % h, [P, VH, PACK], BF16) for h in range(HALVES)]
+        res_words = [keep("res_words%d" % h, [P, VH], U32) for h in range(HALVES)]
+        res_scales = keep("res_scales", [P, V], U8)
+        out_rows = out_0.rearrange("(p t) v -> p t v", t=PACK)
+        out_words = words_of(out_1)
+
+        def half(h):
+            return slice(h * VH, (h + 1) * VH)
+
+        def product(t, h):
+            rows = slice(t * P, (t + 1) * P)
+            bank = psum.tile([P, VH], F32, name="bank")
+            nc.tensor.matmul_mx(
+                out=bank[:],
+                lhsT=cand_w[:, rows].bitcast(FP8X4),
+                lhsT_scale=cand_s[:, rows],
+                rhs=z_words[h][:].bitcast(FP8X4),
+                rhs_scale=z_scales[h][:],
+                start=True,
+                stop=True,
+            )
+            return bank
+
+        for h in range(HALVES):
+            bank = product(0, h)
+            nc.scalar.activation(out=gate[0][:, half(h)], in_=bank[:], func=ACT.Sigmoid, scale=0.0625)
+            nc.vector.tensor_scalar(
+                out=score[0][:, half(h)], in0=bank[:], scalar1=0.0625, scalar2=None, op0=ALU.mult
+            )
+        for t in range(1, PACK):
+            for h in range(HALVES):
+                bank = product(t, h)
+                nc.scalar.activation(out=score[t][:, half(h)], in_=bank[:], func=ACT.Copy, scale=0.0625)
+            for h in range(HALVES):
+                nc.scalar.activation(
+                    out=gate[t][:, half(h)], in_=score[t][:].indirect(entries(n2_sb, h * VH, VH)), func=ACT.Sigmoid
+                )
+
+        def gated(t):
+            nc.vector.tensor_tensor(out=st[t][:], in0=score[t][:], in1=gate[t][:], op=ALU.mult)
+
+        def fetch(t, h):
+            other = ring.tile([P, VH], F32, name="other")
+            nc.vector.tensor_copy(other[:], st[t][:].indirect(entries(n2_sb, h * VH, VH)))
+            return other
+
+        def larger(t, h, other):
+            nc.vector.tensor_tensor(out=res[h][:, t, :], in0=st[t][:, half(h)], in1=other[:], op=ALU.max)
+            nc.sync.dma_start(out=out_rows[:, t, half(h)], in_=res[h][:, t, :])
+
+        def quantize_result(h):
+            nc.vector.quantize_mx(
+                out=res_words[h][:].bitcast(FP8X4),
+                scales=res_scales[:, half(h)],
+                in_=res_bf[h][:].rearrange("p v t -> p (v t)"),
+            )
+            nc.scalar.dma_start(out=out_words[:, half(h)], in_=res_words[h][:].bitcast(I32))
+
+        for h in range(HALVES):
+            nc.vector.tensor_tensor(
+                out=st[0][:, half(h)],
+                in0=gate[0][:].indirect(entries(n2_sb, h * VH, VH)),
+                in1=score[0][:, half(h)],
+                op=ALU.mult,
+            )
+        late = None
+        for t in range(PACK):
+            first = fetch(t, 0)
+            if late is not None:
+                larger(t - 1, 1, late)
+            if t + 1 < PACK:
+                late = fetch(t, 1)
+                larger(t, 0, first)
+                gated(t + 1)
+            else:
+                larger(t, 0, first)
+                nc.scalar.activation(out=res_bf[0][:], in_=res[0][:].rearrange("p t v -> p v t"), func=ACT.Copy)
+                late = fetch(t, 1)
+        larger(PACK - 1, 1, late)
+        nc.vector.tensor_copy(res_bf[1][:], res[1][:].rearrange("p t v -> p v t"))
+        quantize_result(0)
+        quantize_result(1)
+        for q in range(4):
+            queue = nc.sync if q % 2 == 0 else nc.scalar
+            queue.dma_start(
+                out=out_2[0, 4 * q : 4 * q + 4, :].bitcast(I32),
+                in_=res_scales[32 * q : 32 * q + 4, :].bitcast(I32),
+            )

@@ -62,14 +62,14 @@ def tile_picked_candprmstwicp_none_po_kernel(
         nc.vector.memset(xs[:].bitcast(I32), 0)
         nc.vector.memset(ws[:].bitcast(I32), 0)
         nc.sync.dma_start(offs_sb[:], offs)
+        nc.sync.dma_start(out=ww[:].bitcast(I32), in_=words_of(w1_words))
+        load_scale_rows([nc.sync] * 4, xs, x_scales)
+        nc.sync.dma_start(out=xw[:].bitcast(I32), in_=words_of(x_words))
+        load_scale_rows([nc.sync] * 4, ws, w1_scales)
         nc.sync.dma_start(cand_sb[:], cand)
         nc.sync.dma_start(n1_sb[:], n1)
+        nc.sync.dma_start(out=gs_sb[:], in_=gs.rearrange("(p t) o -> p (t o)", t=PACK))
         nc.sync.dma_start(n2_sb[:], n2)
-        nc.sync.dma_start(out=xw[:].bitcast(I32), in_=words_of(x_words))
-        nc.sync.dma_start(out=ww[:].bitcast(I32), in_=words_of(w1_words))
-        load_scale_rows([nc.scalar] * 4, xs, x_scales)
-        load_scale_rows([nc.scalar, nc.scalar, nc.gpsimd, nc.gpsimd], ws, w1_scales)
-        nc.gpsimd.dma_start(out=gs_sb[:], in_=gs.rearrange("(p t) o -> p (t o)", t=PACK))
 
         pick_s = keep("pick_s", [P, S], U8)
         nc.vector.tensor_copy(pick_s[:], xs[:].indirect(offs_sb[:]))
@@ -110,8 +110,7 @@ def tile_picked_candprmstwicp_none_po_kernel(
 
         z_words = [keep("z_words%d" % h, [P, VH], U32) for h in range(HALVES)]
         z_scales = [keep("z_scales%d" % h, [P, VH], U8) for h in range(HALVES)]
-        ms = [keep("ms%d" % h, [P, PACK, VH], F32) for h in range(HALVES)]
-        root = [keep("root%d" % h, [P, VH, PACK], F32) for h in range(HALVES)]
+        z_rows = [keep("z_rows%d" % h, [P, PACK, VH], BF16) for h in range(HALVES)]
         z_bf = [keep("z_bf%d" % h, [P, VH, PACK], BF16) for h in range(HALVES)]
 
         def line_up(h, t):
@@ -124,16 +123,15 @@ def tile_picked_candprmstwicp_none_po_kernel(
 
         def pair_sum(h, t, lined):
             pairs = lined[:].rearrange("p (v two) -> p v two", two=2)
-            nc.vector.scalar_tensor_tensor(
-                out=ms[h][:, t, :], in0=pairs[:, :, 0], scalar=0.1, in1=pairs[:, :, 1], op0=ALU.add, op1=ALU.add
-            )
-
-        def take_root(h):
-            nc.scalar.activation(out=root[h][:], in_=ms[h][:].rearrange("p t v -> p v t"), func=ACT.Sqrt)
+            ms = ring.tile([P, VH], F32, name="ms")
+            nc.gpsimd.tensor_tensor(out=ms[:], in0=pairs[:, :, 0], in1=pairs[:, :, 1], op=ALU.add)
+            root = ring.tile([P, VH], F32, name="root")
+            nc.scalar.activation(out=root[:], in_=ms[:], func=ACT.Sqrt, bias=0.1)
+            nc.scalar.activation(out=z_rows[h][:, t, :], in_=root[:], func=ACT.Copy, scale=gs_sb[:, t : t + 1])
 
         def weigh(h):
-            nc.vector.tensor_tensor(
-                out=z_bf[h][:], in0=root[h][:], in1=gs_sb[:].unsqueeze(1).to_broadcast([P, VH, PACK]), op=ALU.mult
+            nc.vector.tensor_copy(
+                z_bf[h][:].rearrange("p (c i) t -> p c t i", i=4), z_rows[h][:].rearrange("p t (c i) -> p c t i", i=4)
             )
 
         def quantize_z(h):
@@ -152,15 +150,12 @@ def tile_picked_candprmstwicp_none_po_kernel(
                 )
             if before is not None:
                 pair_sum(*before)
-                if before[1] == PACK - 1:
-                    take_root(before[0])
             if (h, t) == (1, 2):
                 weigh(0)
             if (h, t) == (1, 3):
                 quantize_z(0)
             before = (h, t, lined)
         pair_sum(*before)
-        take_root(1)
         cand_w = keep("cand_w", [P, C], U32, "slot_c")
         nc.vector.tensor_copy(cand_w[:].rearrange("p (t m) -> p m t", t=PACK), xw[:].indirect(cand_sb[:]))
         weigh(1)

@@ -21,6 +21,7 @@ LIST_ROWS = 16
 HALVES = 2
 SH = S // HALVES
 VH = V // HALVES
+VQ = VH // 2
 
 
 def entries(lst, first, count):
@@ -46,7 +47,7 @@ def tile_picked_candprmstwicp_none_po_kernel(
         xw = keep("xw", [P, T], U32)
         xs = keep("xs", [P, T], U8)
         ww = keep("ww", [P, H], U32)
-        ws = keep("ws", [P, H], U8, "slot_a")
+        ws = keep("ws", [P, H], U8)
         gs_sb = keep("gs_sb", [P, PACK], F32)
 
         def load_scale_rows(queues, tile, scales):
@@ -75,11 +76,11 @@ def tile_picked_candprmstwicp_none_po_kernel(
         nc.vector.tensor_copy(pick_s[:], xs[:].indirect(offs_sb[:]))
         w_words = keep("w_words", [P, H], U32)
         w_scales = keep("w_scales", [P, H], U8)
-        nc.vector.tensor_copy(
-            w_words[:].bitcast(I32).rearrange("p (t m) -> p t m", t=PACK),
-            ww[:].bitcast(I32).rearrange("p (m t) -> p t m", t=PACK),
+        nc.gpsimd.tensor_copy(
+            w_words[:].rearrange("p (t m) -> p t m", t=PACK),
+            ww[:].rearrange("p (m t) -> p t m", t=PACK),
         )
-        nc.vector.tensor_copy(
+        nc.gpsimd.tensor_copy(
             w_scales[:].rearrange("p (t m) -> p t m", t=PACK),
             ws[:].rearrange("p (m t) -> p t m", t=PACK),
         )
@@ -104,65 +105,73 @@ def tile_picked_candprmstwicp_none_po_kernel(
                 )
                 nc.scalar.activation(out=ysq[t][:, cols], in_=bank[:], func=ACT.Square)
 
-        cand_s_raw = keep("cand_s_raw", [P, C], U8, "slot_a")
+        cand_s_raw = keep("cand_s_raw", [P, C], U8)
         cand_s = keep("cand_s", [P, C], U8)
         nc.vector.tensor_copy(cand_s_raw[:], xs[:].indirect(cand_sb[:]))
 
-        z_words = [keep("z_words%d" % h, [P, VH], U32) for h in range(HALVES)]
-        z_scales = [keep("z_scales%d" % h, [P, VH], U8) for h in range(HALVES)]
+        z_words = keep("z_words", [P, V], U32)
+        z_scales = keep("z_scales", [P, V], U8)
+
+        def half(h):
+            return slice(h * VH, (h + 1) * VH)
+
         z_rows = [keep("z_rows%d" % h, [P, PACK, VH], BF16) for h in range(HALVES)]
         z_bf = [keep("z_bf%d" % h, [P, VH, PACK], BF16) for h in range(HALVES)]
 
-        def line_up(h, t):
-            if (h, t) == (HALVES - 1, PACK - 1):
-                lined = keep("last_lined", [P, SH], F32, "slot_c")
+        def pool_pairs(t, first, count, lined_slot=None, root_slot=None):
+            h, cols = first // VH, slice(first % VH, first % VH + count)
+            if lined_slot is None:
+                lined = ring.tile([P, 2 * count], F32, name="lined")
             else:
-                lined = ring.tile([P, SH], F32, name="lined")
-            nc.vector.tensor_copy(lined[:], ysq[t][:].indirect(entries(n1_sb, h * SH, SH)))
-            return lined
-
-        def pair_sum(h, t, lined):
+                lined = keep("held_lined", [P, 2 * count], F32, lined_slot)
+            nc.vector.tensor_copy(lined[:], ysq[t][:].indirect(entries(n1_sb, 2 * first, 2 * count)))
             pairs = lined[:].rearrange("p (v two) -> p v two", two=2)
-            ms = ring.tile([P, VH], F32, name="ms")
+            ms = ring.tile([P, count], F32, name="ms")
             nc.gpsimd.tensor_tensor(out=ms[:], in0=pairs[:, :, 0], in1=pairs[:, :, 1], op=ALU.add)
-            root = ring.tile([P, VH], F32, name="root")
+            if root_slot is None:
+                root = ring.tile([P, count], F32, name="root")
+            else:
+                root = keep("held_root", [P, count], F32, root_slot)
             nc.scalar.activation(out=root[:], in_=ms[:], func=ACT.Sqrt, bias=0.1)
-            nc.scalar.activation(out=z_rows[h][:, t, :], in_=root[:], func=ACT.Copy, scale=gs_sb[:, t : t + 1])
+            nc.scalar.activation(out=z_rows[h][:, t, cols], in_=root[:], func=ACT.Copy, scale=gs_sb[:, t : t + 1])
 
-        def weigh(h):
-            nc.vector.tensor_copy(
-                z_bf[h][:].rearrange("p (c i) t -> p c t i", i=4), z_rows[h][:].rearrange("p t (c i) -> p c t i", i=4)
+        def weave(engine_copy, woven, rows, first, last):
+            engine_copy(
+                woven[:, first:last, :].rearrange("p (c i) t -> p c t i", i=4),
+                rows[:, :, first:last].rearrange("p t (c i) -> p c t i", i=4),
             )
 
-        def quantize_z(h):
+        def quantize_z(first, count):
+            h, cols = first // VH, slice(first % VH, first % VH + count)
             nc.vector.quantize_mx(
-                out=z_words[h][:].bitcast(FP8X4), scales=z_scales[h][:], in_=z_bf[h][:].rearrange("p v t -> p (v t)")
+                out=z_words[:, first : first + count].bitcast(FP8X4),
+                scales=z_scales[:, first : first + count],
+                in_=z_bf[h][:, cols, :].rearrange("p v t -> p (v t)"),
             )
 
-        steps = [(h, t) for h in range(HALVES) for t in range(PACK)]
-        before = None
-        for h, t in steps:
-            lined = line_up(h, t)
-            if (h, t) == (0, 0):
-                nc.vector.tensor_copy(
-                    cand_s[:].rearrange("p (t m) -> p t m", t=PACK),
-                    cand_s_raw[:].rearrange("p (m t) -> p t m", t=PACK),
-                )
-            if before is not None:
-                pair_sum(*before)
-            if (h, t) == (1, 2):
-                weigh(0)
-            if (h, t) == (1, 3):
-                quantize_z(0)
-            before = (h, t, lined)
-        pair_sum(*before)
+        pool_pairs(0, 0, VH)
+        nc.vector.tensor_copy(
+            cand_s[:].rearrange("p (t m) -> p t m", t=PACK),
+            cand_s_raw[:].rearrange("p (m t) -> p t m", t=PACK),
+        )
+        for t in range(1, PACK):
+            pool_pairs(t, 0, VH)
+        pool_pairs(0, VH, VH)
+        weave(nc.scalar.copy, z_bf[0], z_rows[0], 0, VH)
+        pool_pairs(1, VH, VH)
+        pool_pairs(2, VH, VH, lined_slot="slot_c")
+        quantize_z(0, VH)
+        pool_pairs(3, VH, VQ)
+        pool_pairs(3, VH + VQ, VQ, root_slot="slot_d")
         cand_w = keep("cand_w", [P, C], U32, "slot_c")
         nc.vector.tensor_copy(cand_w[:].rearrange("p (t m) -> p m t", t=PACK), xw[:].indirect(cand_sb[:]))
-        weigh(1)
-        quantize_z(1)
+        weave(nc.vector.tensor_copy, z_bf[1], z_rows[1], 0, VQ)
+        weave(nc.vector.tensor_copy, z_bf[1], z_rows[1], VQ, VH)
+        quantize_z(VH, VQ)
+        quantize_z(VH + VQ, VQ)
 
-        score = [keep("score%d" % t, [P, V], F32) for t in range(PACK)]
-        gate = [keep("gate%d" % t, [P, V], F32) for t in range(PACK)]
+        score = {t: keep("score%d" % t, [P, V], F32) for t in range(1, PACK)}
+        gate = [keep("gate%d" % t, [P, V], F32, "slot_d" if t == 0 else None) for t in range(PACK)]
         st = [keep("st%d" % t, [P, V], F32) for t in range(PACK)]
         res = [keep("res%d" % h, [P, PACK, VH], F32) for h in range(HALVES)]
         res_bf = [keep("res_bf%d" % h, [P, VH, PACK], BF16) for h in range(HALVES)]
@@ -171,33 +180,28 @@ def tile_picked_candprmstwicp_none_po_kernel(
         out_rows = out_0.rearrange("(p t) v -> p t v", t=PACK)
         out_words = words_of(out_1)
 
-        def half(h):
-            return slice(h * VH, (h + 1) * VH)
-
-        def product(t, h):
+        def product(t, cols):
             rows = slice(t * P, (t + 1) * P)
-            bank = psum.tile([P, VH], F32, name="bank")
+            bank = psum.tile([P, cols.stop - cols.start], F32, name="bank")
             nc.tensor.matmul_mx(
                 out=bank[:],
                 lhsT=cand_w[:, rows].bitcast(FP8X4),
                 lhsT_scale=cand_s[:, rows],
-                rhs=z_words[h][:].bitcast(FP8X4),
-                rhs_scale=z_scales[h][:],
+                rhs=z_words[:, cols].bitcast(FP8X4),
+                rhs_scale=z_scales[:, cols],
                 start=True,
                 stop=True,
             )
             return bank
 
+        first_banks = []
         for h in range(HALVES):
-            bank = product(0, h)
+            bank = product(0, half(h))
             nc.scalar.activation(out=gate[0][:, half(h)], in_=bank[:], func=ACT.Sigmoid, scale=0.0625)
-            nc.vector.tensor_scalar(
-                out=score[0][:, half(h)], in0=bank[:], scalar1=0.0625, scalar2=None, op0=ALU.mult
-            )
+            first_banks.append(bank)
         for t in range(1, PACK):
-            for h in range(HALVES):
-                bank = product(t, h)
-                nc.scalar.activation(out=score[t][:, half(h)], in_=bank[:], func=ACT.Copy, scale=0.0625)
+            bank = product(t, slice(0, V))
+            nc.scalar.activation(out=score[t][:], in_=bank[:], func=ACT.Copy, scale=0.0625)
             for h in range(HALVES):
                 nc.scalar.activation(
                     out=gate[t][:, half(h)], in_=score[t][:].indirect(entries(n2_sb, h * VH, VH)), func=ACT.Sigmoid
@@ -223,28 +227,38 @@ def tile_picked_candprmstwicp_none_po_kernel(
             )
             nc.scalar.dma_start(out=out_words[:, half(h)], in_=res_words[h][:].bitcast(I32))
 
+        first_gates = []
         for h in range(HALVES):
-            nc.vector.tensor_tensor(
+            looked_up = ring.tile([P, VH], F32, name="other")
+            nc.vector.tensor_copy(looked_up[:], gate[0][:].indirect(entries(n2_sb, h * VH, VH)))
+            first_gates.append(looked_up)
+        for h in range(HALVES):
+            nc.vector.scalar_tensor_tensor(
                 out=st[0][:, half(h)],
-                in0=gate[0][:].indirect(entries(n2_sb, h * VH, VH)),
-                in1=score[0][:, half(h)],
-                op=ALU.mult,
+                in0=first_banks[h][:],
+                scalar=0.0625,
+                in1=first_gates[h][:],
+                op0=ALU.mult,
+                op1=ALU.mult,
             )
-        late = None
-        for t in range(PACK):
-            first = fetch(t, 0)
-            if late is not None:
-                larger(t - 1, 1, late)
-            if t + 1 < PACK:
-                late = fetch(t, 1)
-                larger(t, 0, first)
-                gated(t + 1)
-            else:
-                larger(t, 0, first)
-                nc.scalar.activation(out=res_bf[0][:], in_=res[0][:].rearrange("p t v -> p v t"), func=ACT.Copy)
-                late = fetch(t, 1)
-        larger(PACK - 1, 1, late)
-        nc.vector.tensor_copy(res_bf[1][:], res[1][:].rearrange("p t v -> p v t"))
+
+        for t in range(PACK - 2):
+            others = [fetch(t, h) for h in range(HALVES)]
+            larger(t, 0, others[0])
+            gated(t + 1)
+            larger(t, 1, others[1])
+        other_2 = fetch(2, 0)
+        gated(3)
+        larger(2, 0, other_2)
+        other_3 = fetch(3, 0)
+        other_2 = fetch(2, 1)
+        larger(3, 0, other_3)
+        weave(nc.scalar.copy, res_bf[0], res[0], 0, VH)
+        other_3 = fetch(3, 1)
+        larger(2, 1, other_2)
+        larger(3, 1, other_3)
+        weave(nc.vector.tensor_copy, res_bf[1], res[1], 0, 160)
+        weave(nc.scalar.copy, res_bf[1], res[1], 160, VH)
         quantize_result(0)
         quantize_result(1)
         for q in range(4):

@@ -17,15 +17,43 @@ ALU = mybir.AluOpType
 
 P = 128
 PACK = 4
+QUADRANTS = 4
 LIST_ROWS = 16
 HALVES = 2
 SH = S // HALVES
 VH = V // HALVES
 VQ = VH // 2
+RUN = 4
+RING_BUFS = 5
+PSUM_BANKS = 8
+VECTOR_SHARE = 160
+PAIR_BIAS = 0.1
+SCORE_SCALE = 0.0625
 
 
-def entries(lst, first, count):
-    return lst[:, first // LIST_ROWS : (first + count) // LIST_ROWS]
+def entries(list_tile, first, count):
+    return list_tile[:, first // LIST_ROWS : (first + count) // LIST_ROWS]
+
+
+def half(h):
+    return slice(h * VH, (h + 1) * VH)
+
+
+def words_of(dram):
+    return dram[0].rearrange("p n t -> p (n t)").bitcast(I32)
+
+
+def deal(engine, dealt, plain):
+    engine.tensor_copy(
+        dealt[:].rearrange("p (t m) -> p t m", t=PACK), plain[:].rearrange("p (m t) -> p t m", t=PACK)
+    )
+
+
+def weave(copy, woven, rows, first, last):
+    copy(
+        woven[:, first:last, :].rearrange("p (c i) t -> p c t i", i=RUN),
+        rows[:, :, first:last].rearrange("p t (c i) -> p c t i", i=RUN),
+    )
 
 
 def tile_picked_candprmstwicp_none_po_kernel(
@@ -34,236 +62,203 @@ def tile_picked_candprmstwicp_none_po_kernel(
     nc = tc.nc
     with ExitStack() as ctx:
         held = ctx.enter_context(tc.tile_pool(name="held", bufs=1))
-        ring = ctx.enter_context(tc.tile_pool(name="ring", bufs=3))
-        psum = ctx.enter_context(tc.psum_pool(name="psum", bufs=8))
+        ring = ctx.enter_context(tc.tile_pool(name="ring", bufs=RING_BUFS))
+        psum = ctx.enter_context(tc.psum_pool(name="psum", bufs=PSUM_BANKS))
 
         def keep(name, shape, dtype, tag=None):
             return held.tile(shape, dtype, name=name, tag=tag or name, align_bytes=64)
+
+        def product(words, scales, t, moving_words, moving_scales):
+            rows = slice(t * P, (t + 1) * P)
+            bank = psum.tile([P, moving_words.shape[1]], F32, name="bank")
+            nc.tensor.matmul_mx(
+                out=bank[:],
+                lhsT=words[:, rows].bitcast(FP8X4),
+                lhsT_scale=scales[:, rows],
+                rhs=moving_words.bitcast(FP8X4),
+                rhs_scale=moving_scales,
+                start=True,
+                stop=True,
+            )
+            return bank
 
         offs_sb = held.tile([P, S // LIST_ROWS], U16, name="offs_sb")
         n1_sb = held.tile([P, S // LIST_ROWS], U16, name="n1_sb")
         cand_sb = held.tile([P, C // LIST_ROWS], U16, name="cand_sb")
         n2_sb = held.tile([P, V // LIST_ROWS], U16, name="n2_sb")
-        xw = keep("xw", [P, T], U32)
-        xs = keep("xs", [P, T], U8)
-        ww = keep("ww", [P, H], U32)
-        ws = keep("ws", [P, H], U8)
+        x_words_sb = keep("x_words_sb", [P, T], U32)
+        x_scales_sb = keep("x_scales_sb", [P, T], U8)
+        w1_words_sb = keep("w1_words_sb", [P, H], U32)
+        w1_scales_sb = keep("w1_scales_sb", [P, H], U8)
         gs_sb = keep("gs_sb", [P, PACK], F32)
 
-        def load_scale_rows(queues, tile, scales):
-            for q in range(4):
-                queues[q].dma_start(
-                    out=tile[32 * q : 32 * q + 4, :].bitcast(I32),
-                    in_=scales[0, 4 * q : 4 * q + 4, :].bitcast(I32),
+        def load_scale_rows(tile, scales):
+            for q in range(QUADRANTS):
+                nc.sync.dma_start(
+                    out=tile[32 * q : 32 * q + 4, :].bitcast(I32), in_=scales[0, 4 * q : 4 * q + 4, :].bitcast(I32)
                 )
 
-        def words_of(dram):
-            return dram[0].rearrange("p n t -> p (n t)").bitcast(I32)
-
-        nc.vector.memset(xs[:].bitcast(I32), 0)
-        nc.vector.memset(ws[:].bitcast(I32), 0)
+        nc.vector.memset(x_scales_sb[:].bitcast(I32), 0)
+        nc.vector.memset(w1_scales_sb[:].bitcast(I32), 0)
         nc.sync.dma_start(offs_sb[:], offs)
-        nc.sync.dma_start(out=ww[:].bitcast(I32), in_=words_of(w1_words))
-        load_scale_rows([nc.sync] * 4, xs, x_scales)
-        nc.sync.dma_start(out=xw[:].bitcast(I32), in_=words_of(x_words))
-        load_scale_rows([nc.sync] * 4, ws, w1_scales)
+        nc.sync.dma_start(out=w1_words_sb[:].bitcast(I32), in_=words_of(w1_words))
+        load_scale_rows(x_scales_sb, x_scales)
+        nc.sync.dma_start(out=x_words_sb[:].bitcast(I32), in_=words_of(x_words))
+        load_scale_rows(w1_scales_sb, w1_scales)
         nc.sync.dma_start(cand_sb[:], cand)
         nc.sync.dma_start(n1_sb[:], n1)
         nc.sync.dma_start(out=gs_sb[:], in_=gs.rearrange("(p t) o -> p (t o)", t=PACK))
         nc.sync.dma_start(n2_sb[:], n2)
 
-        pick_s = keep("pick_s", [P, S], U8)
-        nc.vector.tensor_copy(pick_s[:], xs[:].indirect(offs_sb[:]))
-        w_words = keep("w_words", [P, H], U32)
-        w_scales = keep("w_scales", [P, H], U8)
-        nc.gpsimd.tensor_copy(
-            w_words[:].rearrange("p (t m) -> p t m", t=PACK),
-            ww[:].rearrange("p (m t) -> p t m", t=PACK),
-        )
-        nc.gpsimd.tensor_copy(
-            w_scales[:].rearrange("p (t m) -> p t m", t=PACK),
-            ws[:].rearrange("p (m t) -> p t m", t=PACK),
-        )
-        pick_w = [keep("pick_w0", [P, SH], U32), keep("pick_w1", [P, SH], U32)]
+        pick_scales = keep("pick_scales", [P, S], U8)
+        nc.vector.tensor_copy(pick_scales[:], x_scales_sb[:].indirect(offs_sb[:]))
+        w1_words_dealt = keep("w1_words_dealt", [P, H], U32)
+        w1_scales_dealt = keep("w1_scales_dealt", [P, H], U8)
+        deal(nc.gpsimd, w1_words_dealt, w1_words_sb)
+        deal(nc.gpsimd, w1_scales_dealt, w1_scales_sb)
+        pick_words = [keep("pick_words%d" % h, [P, SH], U32) for h in range(HALVES)]
         for h in range(HALVES):
-            nc.vector.tensor_copy(pick_w[h][:], xw[:].indirect(entries(offs_sb, h * SH, SH)))
+            nc.vector.tensor_copy(pick_words[h][:], x_words_sb[:].indirect(entries(offs_sb, h * SH, SH)))
 
-        ysq = [keep("ysq%d" % t, [P, S], F32) for t in range(PACK)]
+        y_squared = [keep("y_squared%d" % t, [P, S], F32) for t in range(PACK)]
         for t in range(PACK):
-            rows = slice(t * P, (t + 1) * P)
             for h in range(HALVES):
                 cols = slice(h * SH, (h + 1) * SH)
-                bank = psum.tile([P, SH], F32, name="bank")
-                nc.tensor.matmul_mx(
-                    out=bank[:],
-                    lhsT=w_words[:, rows].bitcast(FP8X4),
-                    lhsT_scale=w_scales[:, rows],
-                    rhs=pick_w[h][:].bitcast(FP8X4),
-                    rhs_scale=pick_s[:, cols],
-                    start=True,
-                    stop=True,
-                )
-                nc.scalar.activation(out=ysq[t][:, cols], in_=bank[:], func=ACT.Square)
+                bank = product(w1_words_dealt, w1_scales_dealt, t, pick_words[h][:], pick_scales[:, cols])
+                nc.scalar.activation(out=y_squared[t][:, cols], in_=bank[:], func=ACT.Square)
 
-        cand_s_raw = keep("cand_s_raw", [P, C], U8)
-        cand_s = keep("cand_s", [P, C], U8)
-        nc.vector.tensor_copy(cand_s_raw[:], xs[:].indirect(cand_sb[:]))
+        cand_scales = keep("cand_scales", [P, C], U8)
+        cand_scales_dealt = keep("cand_scales_dealt", [P, C], U8)
+        nc.vector.tensor_copy(cand_scales[:], x_scales_sb[:].indirect(cand_sb[:]))
 
         z_words = keep("z_words", [P, V], U32)
         z_scales = keep("z_scales", [P, V], U8)
-
-        def half(h):
-            return slice(h * VH, (h + 1) * VH)
-
         z_rows = [keep("z_rows%d" % h, [P, PACK, VH], BF16) for h in range(HALVES)]
-        z_bf = [keep("z_bf%d" % h, [P, VH, PACK], BF16) for h in range(HALVES)]
+        z_woven = [keep("z_woven%d" % h, [P, VH, PACK], BF16) for h in range(HALVES)]
 
-        def pool_pairs(t, first, count, lined_slot=None, root_slot=None):
+        def pool_pairs(t, first, count, lined_tag=None, root_tag=None):
             h, cols = first // VH, slice(first % VH, first % VH + count)
-            if lined_slot is None:
+            if lined_tag is None:
                 lined = ring.tile([P, 2 * count], F32, name="lined")
             else:
-                lined = keep("held_lined", [P, 2 * count], F32, lined_slot)
-            nc.vector.tensor_copy(lined[:], ysq[t][:].indirect(entries(n1_sb, 2 * first, 2 * count)))
+                lined = keep("held_lined", [P, 2 * count], F32, lined_tag)
+            nc.vector.tensor_copy(lined[:], y_squared[t][:].indirect(entries(n1_sb, 2 * first, 2 * count)))
             pairs = lined[:].rearrange("p (v two) -> p v two", two=2)
-            ms = ring.tile([P, count], F32, name="ms")
-            nc.gpsimd.tensor_tensor(out=ms[:], in0=pairs[:, :, 0], in1=pairs[:, :, 1], op=ALU.add)
-            if root_slot is None:
+            pair_sum = ring.tile([P, count], F32, name="pair_sum")
+            nc.gpsimd.tensor_tensor(out=pair_sum[:], in0=pairs[:, :, 0], in1=pairs[:, :, 1], op=ALU.add)
+            if root_tag is None:
                 root = ring.tile([P, count], F32, name="root")
             else:
-                root = keep("held_root", [P, count], F32, root_slot)
-            nc.scalar.activation(out=root[:], in_=ms[:], func=ACT.Sqrt, bias=0.1)
+                root = keep("held_root", [P, count], F32, root_tag)
+            nc.scalar.activation(out=root[:], in_=pair_sum[:], func=ACT.Sqrt, bias=PAIR_BIAS)
             nc.scalar.activation(out=z_rows[h][:, t, cols], in_=root[:], func=ACT.Copy, scale=gs_sb[:, t : t + 1])
-
-        def weave(engine_copy, woven, rows, first, last):
-            engine_copy(
-                woven[:, first:last, :].rearrange("p (c i) t -> p c t i", i=4),
-                rows[:, :, first:last].rearrange("p t (c i) -> p c t i", i=4),
-            )
 
         def quantize_z(first, count):
             h, cols = first // VH, slice(first % VH, first % VH + count)
             nc.vector.quantize_mx(
                 out=z_words[:, first : first + count].bitcast(FP8X4),
                 scales=z_scales[:, first : first + count],
-                in_=z_bf[h][:, cols, :].rearrange("p v t -> p (v t)"),
+                in_=z_woven[h][:, cols, :].rearrange("p v t -> p (v t)"),
             )
 
+        last = PACK - 1
         pool_pairs(0, 0, VH)
-        nc.vector.tensor_copy(
-            cand_s[:].rearrange("p (t m) -> p t m", t=PACK),
-            cand_s_raw[:].rearrange("p (m t) -> p t m", t=PACK),
-        )
+        deal(nc.vector, cand_scales_dealt, cand_scales)
         for t in range(1, PACK):
             pool_pairs(t, 0, VH)
         pool_pairs(0, VH, VH)
-        weave(nc.scalar.copy, z_bf[0], z_rows[0], 0, VH)
+        weave(nc.scalar.copy, z_woven[0], z_rows[0], 0, VH)
         pool_pairs(1, VH, VH)
-        pool_pairs(2, VH, VH, lined_slot="slot_c")
+        pool_pairs(2, VH, VH, lined_tag="then_cand_words")
         quantize_z(0, VH)
-        pool_pairs(3, VH, VQ)
-        pool_pairs(3, VH + VQ, VQ, root_slot="slot_d")
-        cand_w = keep("cand_w", [P, C], U32, "slot_c")
-        nc.vector.tensor_copy(cand_w[:].rearrange("p (t m) -> p m t", t=PACK), xw[:].indirect(cand_sb[:]))
-        weave(nc.vector.tensor_copy, z_bf[1], z_rows[1], 0, VQ)
-        weave(nc.vector.tensor_copy, z_bf[1], z_rows[1], VQ, VH)
+        pool_pairs(last, VH, VQ)
+        pool_pairs(last, VH + VQ, VQ, root_tag="then_gate0")
+
+        cand_words_dealt = keep("cand_words_dealt", [P, C], U32, "then_cand_words")
+        nc.vector.tensor_copy(
+            cand_words_dealt[:].rearrange("p (t m) -> p m t", t=PACK), x_words_sb[:].indirect(cand_sb[:])
+        )
+
+        weave(nc.vector.tensor_copy, z_woven[1], z_rows[1], 0, VQ)
+        weave(nc.vector.tensor_copy, z_woven[1], z_rows[1], VQ, VH)
         quantize_z(VH, VQ)
         quantize_z(VH + VQ, VQ)
 
-        score = {t: keep("score%d" % t, [P, V], F32) for t in range(1, PACK)}
-        gate = [keep("gate%d" % t, [P, V], F32, "slot_d" if t == 0 else None) for t in range(PACK)]
-        st = [keep("st%d" % t, [P, V], F32) for t in range(PACK)]
-        res = [keep("res%d" % h, [P, PACK, VH], F32) for h in range(HALVES)]
-        res_bf = [keep("res_bf%d" % h, [P, VH, PACK], BF16) for h in range(HALVES)]
-        res_words = [keep("res_words%d" % h, [P, VH], U32) for h in range(HALVES)]
-        res_scales = keep("res_scales", [P, V], U8)
-        out_rows = out_0.rearrange("(p t) v -> p t v", t=PACK)
-        out_words = words_of(out_1)
+        def scores(t, cols):
+            return product(cand_words_dealt, cand_scales_dealt, t, z_words[:, cols], z_scales[:, cols])
 
-        def product(t, cols):
-            rows = slice(t * P, (t + 1) * P)
-            bank = psum.tile([P, cols.stop - cols.start], F32, name="bank")
-            nc.tensor.matmul_mx(
-                out=bank[:],
-                lhsT=cand_w[:, rows].bitcast(FP8X4),
-                lhsT_scale=cand_s[:, rows],
-                rhs=z_words[:, cols].bitcast(FP8X4),
-                rhs_scale=z_scales[:, cols],
-                start=True,
-                stop=True,
-            )
-            return bank
-
-        first_banks = []
+        sigmoid_0 = keep("sigmoid_0", [P, V], F32, "then_gate0")
+        banks_0 = []
         for h in range(HALVES):
-            bank = product(0, half(h))
-            nc.scalar.activation(out=gate[0][:, half(h)], in_=bank[:], func=ACT.Sigmoid, scale=0.0625)
-            first_banks.append(bank)
+            banks_0.append(scores(0, half(h)))
+            nc.scalar.activation(out=sigmoid_0[:, half(h)], in_=banks_0[h][:], func=ACT.Sigmoid, scale=SCORE_SCALE)
+        score = {t: keep("score%d" % t, [P, V], F32) for t in range(1, PACK)}
+        gate = {t: keep("gate%d" % t, [P, V], F32) for t in range(1, PACK)}
         for t in range(1, PACK):
-            bank = product(t, slice(0, V))
-            nc.scalar.activation(out=score[t][:], in_=bank[:], func=ACT.Copy, scale=0.0625)
+            bank = scores(t, slice(0, V))
+            nc.scalar.activation(out=score[t][:], in_=bank[:], func=ACT.Copy, scale=SCORE_SCALE)
             for h in range(HALVES):
                 nc.scalar.activation(
                     out=gate[t][:, half(h)], in_=score[t][:].indirect(entries(n2_sb, h * VH, VH)), func=ACT.Sigmoid
                 )
 
-        def gated(t):
-            nc.vector.tensor_tensor(out=st[t][:], in0=score[t][:], in1=gate[t][:], op=ALU.mult)
+        result = [keep("result%d" % h, [P, PACK, VH], F32) for h in range(HALVES)]
+        result_woven = [keep("result_woven%d" % h, [P, VH, PACK], BF16) for h in range(HALVES)]
+        result_words = [keep("result_words%d" % h, [P, VH], U32) for h in range(HALVES)]
+        result_scales = keep("result_scales", [P, V], U8)
+        out_rows = out_0.rearrange("(p t) v -> p t v", t=PACK)
 
-        def fetch(t, h):
-            other = ring.tile([P, VH], F32, name="other")
-            nc.vector.tensor_copy(other[:], st[t][:].indirect(entries(n2_sb, h * VH, VH)))
-            return other
+        def new_st(t):
+            return keep("st%d" % t, [P, V], F32, "st_buffer%d" % (t % 2))
 
-        def larger(t, h, other):
-            nc.vector.tensor_tensor(out=res[h][:, t, :], in0=st[t][:, half(h)], in1=other[:], op=ALU.max)
-            nc.sync.dma_start(out=out_rows[:, t, half(h)], in_=res[h][:, t, :])
+        def fetch(window, h):
+            fetched = ring.tile([P, VH], F32, name="fetched")
+            nc.vector.tensor_copy(fetched[:], window[:].indirect(entries(n2_sb, h * VH, VH)))
+            return fetched
 
-        def quantize_result(h):
-            nc.vector.quantize_mx(
-                out=res_words[h][:].bitcast(FP8X4),
-                scales=res_scales[:, half(h)],
-                in_=res_bf[h][:].rearrange("p v t -> p (v t)"),
-            )
-            nc.scalar.dma_start(out=out_words[:, half(h)], in_=res_words[h][:].bitcast(I32))
+        def gated(engine, t, h):
+            engine.tensor_tensor(out=st[t][:, half(h)], in0=score[t][:, half(h)], in1=gate[t][:, half(h)], op=ALU.mult)
 
-        first_gates = []
-        for h in range(HALVES):
-            looked_up = ring.tile([P, VH], F32, name="other")
-            nc.vector.tensor_copy(looked_up[:], gate[0][:].indirect(entries(n2_sb, h * VH, VH)))
-            first_gates.append(looked_up)
+        def larger(t, h, fetched):
+            nc.vector.tensor_tensor(out=result[h][:, t, :], in0=st[t][:, half(h)], in1=fetched[:], op=ALU.max)
+            nc.sync.dma_start(out=out_rows[:, t, half(h)], in_=result[h][:, t, :])
+
+        st = {0: new_st(0)}
+        gates_0 = [fetch(sigmoid_0, h) for h in range(HALVES)]
         for h in range(HALVES):
             nc.vector.scalar_tensor_tensor(
                 out=st[0][:, half(h)],
-                in0=first_banks[h][:],
-                scalar=0.0625,
-                in1=first_gates[h][:],
+                in0=banks_0[h][:],
+                scalar=SCORE_SCALE,
+                in1=gates_0[h][:],
                 op0=ALU.mult,
                 op1=ALU.mult,
             )
+        for t in range(last):
+            st[t + 1] = new_st(t + 1)
+            gated(nc.gpsimd, t + 1, 0)
+            partners = [fetch(st[t], h) for h in range(HALVES)]
+            larger(t, 0, partners[0])
+            gated(nc.vector, t + 1, 1)
+            if t + 1 == last:
+                last_partners = fetch(st[last], 0)
+            larger(t, 1, partners[1])
+        larger(last, 0, last_partners)
+        weave(nc.scalar.copy, result_woven[0], result[0], 0, VH)
+        larger(last, 1, fetch(st[last], 1))
+        weave(nc.vector.tensor_copy, result_woven[1], result[1], 0, VECTOR_SHARE)
+        weave(nc.scalar.copy, result_woven[1], result[1], VECTOR_SHARE, VH)
 
-        for t in range(PACK - 2):
-            others = [fetch(t, h) for h in range(HALVES)]
-            larger(t, 0, others[0])
-            gated(t + 1)
-            larger(t, 1, others[1])
-        other_2 = fetch(2, 0)
-        gated(3)
-        larger(2, 0, other_2)
-        other_3 = fetch(3, 0)
-        other_2 = fetch(2, 1)
-        larger(3, 0, other_3)
-        weave(nc.scalar.copy, res_bf[0], res[0], 0, VH)
-        other_3 = fetch(3, 1)
-        larger(2, 1, other_2)
-        larger(3, 1, other_3)
-        weave(nc.vector.tensor_copy, res_bf[1], res[1], 0, 160)
-        weave(nc.scalar.copy, res_bf[1], res[1], 160, VH)
-        quantize_result(0)
-        quantize_result(1)
-        for q in range(4):
+        for h in range(HALVES):
+            nc.vector.quantize_mx(
+                out=result_words[h][:].bitcast(FP8X4),
+                scales=result_scales[:, half(h)],
+                in_=result_woven[h][:].rearrange("p v t -> p (v t)"),
+            )
+            nc.scalar.dma_start(out=words_of(out_1)[:, half(h)], in_=result_words[h][:].bitcast(I32))
+        for q in range(QUADRANTS):
             queue = nc.sync if q % 2 == 0 else nc.scalar
             queue.dma_start(
                 out=out_2[0, 4 * q : 4 * q + 4, :].bitcast(I32),
-                in_=res_scales[32 * q : 32 * q + 4, :].bitcast(I32),
+                in_=result_scales[32 * q : 32 * q + 4, :].bitcast(I32),
             )

from contextlib import ExitStack

import concourse.mybir as mybir

K, T, S, V, H, C = 512, 2048, 1024, 512, 512, 512
FLOPS = 2 * K * H * S + 2 * K * C * V

F32 = mybir.dt.float32
BF16 = mybir.dt.bfloat16
I32 = mybir.dt.int32
U32 = mybir.dt.uint32
U16 = mybir.dt.uint16
U8 = mybir.dt.uint8
FP8X4 = mybir.dt.float8_e4m3fn_x4
ACT = mybir.ActivationFunctionType
ALU = mybir.AluOpType

P = 128
PACK = 4
QUADRANTS = 4
LIST_ROWS = 16
HALVES = 2
SH = S // HALVES
VH = V // HALVES
VQ = VH // 2
RUN = 4
RING_BUFS = 5
PSUM_BANKS = 8
VECTOR_SHARE = 160
PAIR_BIAS = 0.1
SCORE_SCALE = 0.0625


def entries(list_tile, first, count):
    return list_tile[:, first // LIST_ROWS : (first + count) // LIST_ROWS]


def half(h):
    return slice(h * VH, (h + 1) * VH)


def words_of(dram):
    return dram[0].rearrange("p n t -> p (n t)").bitcast(I32)


def deal(engine, dealt, plain):
    engine.tensor_copy(
        dealt[:].rearrange("p (t m) -> p t m", t=PACK), plain[:].rearrange("p (m t) -> p t m", t=PACK)
    )


def weave(copy, woven, rows, first, last):
    copy(
        woven[:, first:last, :].rearrange("p (c i) t -> p c t i", i=RUN),
        rows[:, :, first:last].rearrange("p t (c i) -> p c t i", i=RUN),
    )


def tile_picked_candprmstwicp_none_po_kernel(
    tc, x_words, x_scales, w1_words, w1_scales, gs, offs, n1, cand, n2, out_0, out_1, out_2
):
    nc = tc.nc
    with ExitStack() as ctx:
        held = ctx.enter_context(tc.tile_pool(name="held", bufs=1))
        ring = ctx.enter_context(tc.tile_pool(name="ring", bufs=RING_BUFS))
        psum = ctx.enter_context(tc.psum_pool(name="psum", bufs=PSUM_BANKS))

        def keep(name, shape, dtype, tag=None):
            return held.tile(shape, dtype, name=name, tag=tag or name, align_bytes=64)

        def product(words, scales, t, moving_words, moving_scales):
            rows = slice(t * P, (t + 1) * P)
            bank = psum.tile([P, moving_words.shape[1]], F32, name="bank")
            nc.tensor.matmul_mx(
                out=bank[:],
                lhsT=words[:, rows].bitcast(FP8X4),
                lhsT_scale=scales[:, rows],
                rhs=moving_words.bitcast(FP8X4),
                rhs_scale=moving_scales,
                start=True,
                stop=True,
            )
            return bank

        offs_sb = held.tile([P, S // LIST_ROWS], U16, name="offs_sb")
        n1_sb = held.tile([P, S // LIST_ROWS], U16, name="n1_sb")
        cand_sb = held.tile([P, C // LIST_ROWS], U16, name="cand_sb")
        n2_sb = held.tile([P, V // LIST_ROWS], U16, name="n2_sb")
        x_words_sb = keep("x_words_sb", [P, T], U32)
        x_scales_sb = keep("x_scales_sb", [P, T], U8)
        w1_words_sb = keep("w1_words_sb", [P, H], U32)
        w1_scales_sb = keep("w1_scales_sb", [P, H], U8)
        gs_sb = keep("gs_sb", [P, PACK], F32)

        def load_scale_rows(tile, scales):
            for q in range(QUADRANTS):
                nc.sync.dma_start(
                    out=tile[32 * q : 32 * q + 4, :].bitcast(I32), in_=scales[0, 4 * q : 4 * q + 4, :].bitcast(I32)
                )

        nc.vector.memset(x_scales_sb[:].bitcast(I32), 0)
        nc.vector.memset(w1_scales_sb[:].bitcast(I32), 0)
        nc.sync.dma_start(offs_sb[:], offs)
        nc.sync.dma_start(out=w1_words_sb[:].bitcast(I32), in_=words_of(w1_words))
        load_scale_rows(x_scales_sb, x_scales)
        nc.sync.dma_start(out=x_words_sb[:].bitcast(I32), in_=words_of(x_words))
        load_scale_rows(w1_scales_sb, w1_scales)
        nc.sync.dma_start(cand_sb[:], cand)
        nc.sync.dma_start(n1_sb[:], n1)
        nc.sync.dma_start(out=gs_sb[:], in_=gs.rearrange("(p t) o -> p (t o)", t=PACK))
        nc.sync.dma_start(n2_sb[:], n2)

        pick_scales = keep("pick_scales", [P, S], U8)
        nc.vector.tensor_copy(pick_scales[:], x_scales_sb[:].indirect(offs_sb[:]))
        w1_words_dealt = keep("w1_words_dealt", [P, H], U32)
        w1_scales_dealt = keep("w1_scales_dealt", [P, H], U8)
        deal(nc.gpsimd, w1_words_dealt, w1_words_sb)
        deal(nc.gpsimd, w1_scales_dealt, w1_scales_sb)
        pick_words = [keep("pick_words%d" % h, [P, SH], U32) for h in range(HALVES)]
        for h in range(HALVES):
            nc.vector.tensor_copy(pick_words[h][:], x_words_sb[:].indirect(entries(offs_sb, h * SH, SH)))

        y_squared = [keep("y_squared%d" % t, [P, S], F32) for t in range(PACK)]
        for t in range(PACK):
            for h in range(HALVES):
                cols = slice(h * SH, (h + 1) * SH)
                bank = product(w1_words_dealt, w1_scales_dealt, t, pick_words[h][:], pick_scales[:, cols])
                nc.scalar.activation(out=y_squared[t][:, cols], in_=bank[:], func=ACT.Square)

        cand_scales = keep("cand_scales", [P, C], U8)
        cand_scales_dealt = keep("cand_scales_dealt", [P, C], U8)
        nc.vector.tensor_copy(cand_scales[:], x_scales_sb[:].indirect(cand_sb[:]))

        z_words = keep("z_words", [P, V], U32)
        z_scales = keep("z_scales", [P, V], U8)
        z_rows = [keep("z_rows%d" % h, [P, PACK, VH], BF16) for h in range(HALVES)]
        z_woven = [keep("z_woven%d" % h, [P, VH, PACK], BF16) for h in range(HALVES)]

        def pool_pairs(t, first, count, lined_tag=None, root_tag=None):
            h, cols = first // VH, slice(first % VH, first % VH + count)
            if lined_tag is None:
                lined = ring.tile([P, 2 * count], F32, name="lined")
            else:
                lined = keep("held_lined", [P, 2 * count], F32, lined_tag)
            nc.vector.tensor_copy(lined[:], y_squared[t][:].indirect(entries(n1_sb, 2 * first, 2 * count)))
            pairs = lined[:].rearrange("p (v two) -> p v two", two=2)
            pair_sum = ring.tile([P, count], F32, name="pair_sum")
            nc.gpsimd.tensor_tensor(out=pair_sum[:], in0=pairs[:, :, 0], in1=pairs[:, :, 1], op=ALU.add)
            if root_tag is None:
                root = ring.tile([P, count], F32, name="root")
            else:
                root = keep("held_root", [P, count], F32, root_tag)
            nc.scalar.activation(out=root[:], in_=pair_sum[:], func=ACT.Sqrt, bias=PAIR_BIAS)
            nc.scalar.activation(out=z_rows[h][:, t, cols], in_=root[:], func=ACT.Copy, scale=gs_sb[:, t : t + 1])

        def quantize_z(first, count):
            h, cols = first // VH, slice(first % VH, first % VH + count)
            nc.vector.quantize_mx(
                out=z_words[:, first : first + count].bitcast(FP8X4),
                scales=z_scales[:, first : first + count],
                in_=z_woven[h][:, cols, :].rearrange("p v t -> p (v t)"),
            )

        last = PACK - 1
        pool_pairs(0, 0, VH)
        deal(nc.vector, cand_scales_dealt, cand_scales)
        for t in range(1, PACK):
            pool_pairs(t, 0, VH)
        pool_pairs(0, VH, VH)
        weave(nc.scalar.copy, z_woven[0], z_rows[0], 0, VH)
        pool_pairs(1, VH, VH)
        pool_pairs(2, VH, VH, lined_tag="then_cand_words")
        quantize_z(0, VH)
        pool_pairs(last, VH, VQ)
        pool_pairs(last, VH + VQ, VQ, root_tag="then_gate0")

        cand_words_dealt = keep("cand_words_dealt", [P, C], U32, "then_cand_words")
        nc.vector.tensor_copy(
            cand_words_dealt[:].rearrange("p (t m) -> p m t", t=PACK), x_words_sb[:].indirect(cand_sb[:])
        )

        weave(nc.vector.tensor_copy, z_woven[1], z_rows[1], 0, VQ)
        weave(nc.vector.tensor_copy, z_woven[1], z_rows[1], VQ, VH)
        quantize_z(VH, VQ)
        quantize_z(VH + VQ, VQ)

        def scores(t, cols):
            return product(cand_words_dealt, cand_scales_dealt, t, z_words[:, cols], z_scales[:, cols])

        sigmoid_0 = keep("sigmoid_0", [P, V], F32, "then_gate0")
        banks_0 = []
        for h in range(HALVES):
            banks_0.append(scores(0, half(h)))
            nc.scalar.activation(out=sigmoid_0[:, half(h)], in_=banks_0[h][:], func=ACT.Sigmoid, scale=SCORE_SCALE)
        score = {t: keep("score%d" % t, [P, V], F32) for t in range(1, PACK)}
        gate = {t: keep("gate%d" % t, [P, V], F32) for t in range(1, PACK)}
        for t in range(1, PACK):
            bank = scores(t, slice(0, V))
            nc.scalar.activation(out=score[t][:], in_=bank[:], func=ACT.Copy, scale=SCORE_SCALE)
            for h in range(HALVES):
                nc.scalar.activation(
                    out=gate[t][:, half(h)], in_=score[t][:].indirect(entries(n2_sb, h * VH, VH)), func=ACT.Sigmoid
                )

        result = [keep("result%d" % h, [P, PACK, VH], F32) for h in range(HALVES)]
        result_woven = [keep("result_woven%d" % h, [P, VH, PACK], BF16) for h in range(HALVES)]
        result_words = [keep("result_words%d" % h, [P, VH], U32) for h in range(HALVES)]
        result_scales = keep("result_scales", [P, V], U8)
        out_rows = out_0.rearrange("(p t) v -> p t v", t=PACK)

        def new_st(t):
            return keep("st%d" % t, [P, V], F32, "st_buffer%d" % (t % 2))

        def fetch(window, h):
            fetched = ring.tile([P, VH], F32, name="fetched")
            nc.vector.tensor_copy(fetched[:], window[:].indirect(entries(n2_sb, h * VH, VH)))
            return fetched

        def gated(engine, t, h):
            engine.tensor_tensor(out=st[t][:, half(h)], in0=score[t][:, half(h)], in1=gate[t][:, half(h)], op=ALU.mult)

        def larger(t, h, fetched):
            nc.vector.tensor_tensor(out=result[h][:, t, :], in0=st[t][:, half(h)], in1=fetched[:], op=ALU.max)
            nc.sync.dma_start(out=out_rows[:, t, half(h)], in_=result[h][:, t, :])

        st = {0: new_st(0)}
        gates_0 = [fetch(sigmoid_0, h) for h in range(HALVES)]
        for h in range(HALVES):
            nc.vector.scalar_tensor_tensor(
                out=st[0][:, half(h)],
                in0=banks_0[h][:],
                scalar=SCORE_SCALE,
                in1=gates_0[h][:],
                op0=ALU.mult,
                op1=ALU.mult,
            )
        for t in range(last):
            st[t + 1] = new_st(t + 1)
            gated(nc.gpsimd, t + 1, 0)
            partners = [fetch(st[t], h) for h in range(HALVES)]
            larger(t, 0, partners[0])
            gated(nc.vector, t + 1, 1)
            if t + 1 == last:
                last_partners = fetch(st[last], 0)
            larger(t, 1, partners[1])
        larger(last, 0, last_partners)
        weave(nc.scalar.copy, result_woven[0], result[0], 0, VH)
        larger(last, 1, fetch(st[last], 1))
        weave(nc.vector.tensor_copy, result_woven[1], result[1], 0, VECTOR_SHARE)
        weave(nc.scalar.copy, result_woven[1], result[1], VECTOR_SHARE, VH)

        for h in range(HALVES):
            nc.vector.quantize_mx(
                out=result_words[h][:].bitcast(FP8X4),
                scales=result_scales[:, half(h)],
                in_=result_woven[h][:].rearrange("p v t -> p (v t)"),
            )
            nc.scalar.dma_start(out=words_of(out_1)[:, half(h)], in_=result_words[h][:].bitcast(I32))
        for q in range(QUADRANTS):
            queue = nc.sync if q % 2 == 0 else nc.scalar
            queue.dma_start(
                out=out_2[0, 4 * q : 4 * q + 4, :].bitcast(I32),
                in_=result_scales[32 * q : 32 * q + 4, :].bitcast(I32),
            )
